import numpy as np
import ml_dtypes


def mxq(x, axis, fmt="e4m3"):
    dtype, down = {"e4m3": (ml_dtypes.float8_e4m3fn, 7), "e5m2": (ml_dtypes.float8_e5m2, 14)}[fmt]
    v = np.moveaxis(np.asarray(x, np.float32).astype(ml_dtypes.bfloat16).astype(np.float64), axis, -1)
    blocks = v.reshape(v.shape[:-1] + (-1, 32))
    amax = np.abs(blocks).max(-1, keepdims=True)
    byte = np.maximum(np.where(amax > 0, np.frexp(amax)[1] - 1 + 127, 0) - down, 1)
    scale = np.exp2(byte - 127.0)
    codes = (blocks / scale).astype(np.float32).astype(dtype).astype(np.float64)
    return np.moveaxis((codes * scale).reshape(v.shape), -1, axis)


WIDE = False


def mx_kscale(k):
    if not WIDE:
        return np.ones(k)
    levels = np.array([10, -10, 5, -5, 0])
    if k % 512:
        return np.exp2(np.random.permutation(np.resize(levels, k // 32))).repeat(32)
    a = np.empty((k // 512, 16))
    for p in range(k // 512):
        a[p, :8] = np.random.permutation(np.resize(levels, 8))
        for g in range(8):
            far = levels[np.abs(levels - a[p, g]) >= 10]
            a[p, g + 8] = far[np.random.randint(len(far))]
    return np.exp2(a.ravel()).repeat(32)


def f64(x):
    return np.asarray(x).astype(np.float64)


def striped(idx):
    return np.tile(idx.reshape(-1, 16).T, (8, 1)).astype(np.uint16)


def unstriped(offs):
    return offs[:16].T.reshape(-1).astype(np.int64)


def pack_weight(w):
    k, n = w.shape
    w = f64(np.asarray(w, np.float32).astype(ml_dtypes.bfloat16)).reshape(k // 32, 32, n)
    amax = np.abs(w).max(1)
    byte = np.clip(np.where(amax > 0, np.frexp(amax)[1] - 1 + 127 - 7, 1), 1, 254)
    scaled = (w * np.exp2(127.0 - byte)[:, None, :]).reshape(k, n).astype(np.float32)
    words = np.ascontiguousarray(scaled.reshape(k // 512, 128, 4, n).transpose(0, 1, 3, 2)).astype(ml_dtypes.float8_e4m3fn).view(np.uint8)
    return words, np.ascontiguousarray(byte.astype(np.uint8).reshape(k // 512, 16, n))


def unpack_weight(words, scales):
    g, p, n, _ = words.shape
    vals = np.ascontiguousarray(words).view(ml_dtypes.float8_e4m3fn).astype(np.float64) * np.repeat(np.exp2(scales.astype(np.float64) - 127.0), 8, axis=1)[..., None]
    return vals.transpose(0, 1, 3, 2).reshape(g * 512, n)


def planes(y):
    n, m = y.shape
    v = y.astype(np.float32).astype(ml_dtypes.bfloat16).astype(np.float64).reshape(n // 32, 32, m)
    top = np.abs(v).max(1)
    byte = np.clip(np.where(top > 0, np.frexp(top)[1] - 1 + 127 - 7, 1), 1, 254)
    codes = (v * np.exp2(127.0 - byte)[:, None, :]).reshape(n, m).astype(np.float32).astype(ml_dtypes.float8_e4m3fn).view(np.uint8)
    words = codes.reshape(n // 512, 128, 4, m).transpose(0, 1, 3, 2)
    return np.ascontiguousarray(words), np.ascontiguousarray(byte.astype(np.uint8).reshape(n // 512, 16, m))


K, T, S, N, W, G = 512, 2048, 512, 512, 2048, 1024


def setup_inputs():
    n = np.random.standard_normal
    s = mx_kscale(K)[:, None]
    packed_xT = pack_weight(n((K, T)) * s)
    packed_eT = pack_weight(n((K, W)) * s)
    packed_dT = pack_weight(n((K, G)) * s)
    return {
        "x_words": packed_xT[0],
        "x_scales": packed_xT[1],
        "e_words": packed_eT[0],
        "e_scales": packed_eT[1],
        "d_words": packed_dT[0],
        "d_scales": packed_dT[1],
        "w1": (n((K, N)) / np.sqrt(K) / s).astype(np.float32),
        "w2": (n((K, N)) / np.sqrt(K) / s).astype(np.float32),
        "w3": (n((K, N)) / np.sqrt(K) / s).astype(np.float32),
        "att": (0.5 * n((N, 1))).astype(np.float32),
        "offs": striped(np.random.permutation(T)[:S]),
        "item": striped(np.random.permutation(W)[:S]),
        "cxt": striped(np.random.permutation(G)[:S]),
    }


def reference(x_words, x_scales, e_words, e_scales, d_words, d_scales, w1, w2, w3, att, offs, item, cxt):
    xq = unpack_weight(x_words, x_scales)[:, unstriped(offs)]
    y0 = mxq(f64(w1), 0, "e4m3").T @ xq
    e_item = unpack_weight(e_words, e_scales)[:, unstriped(item)]
    y1 = mxq(f64(w2), 0, "e4m3").T @ e_item
    p01 = y0 * y1
    e0 = np.exp(np.tanh(f64(att) * p01))
    d_cxt = unpack_weight(d_words, d_scales)[:, unstriped(cxt)]
    y2 = mxq(f64(w3), 0, "e4m3").T @ d_cxt
    p02 = y0 * y2
    e1 = np.exp(np.tanh(f64(att) * p02))
    p12 = y1 * y2
    e2 = np.exp(np.tanh(f64(att) * p12))
    num = p01 * e0 + p02 * e1 + p12 * e2
    den = e0 + e1 + e2
    out_0 = num / den
    return (out_0,) + planes(out_0)

@@ -1,0 +1,272 @@
+from contextlib import ExitStack
+
+import concourse.mybir as mybir
+from concourse.masks import make_identity
+
+F32 = mybir.dt.float32
+BF16 = mybir.dt.bfloat16
+I32 = mybir.dt.int32
+U32 = mybir.dt.uint32
+U16 = mybir.dt.uint16
+U8 = mybir.dt.uint8
+FP8X4 = mybir.dt.float8_e4m3fn_x4
+ACT = mybir.ActivationFunctionType
+MULT = mybir.AluOpType.mult
+ADD = mybir.AluOpType.add
+
+P = 128
+PACK = 4
+K = 512
+N = 512
+S = 512
+HALF = S // 2
+FLOPS = 3 * 2 * K * N * S
+OPT = {"c1":"S","c3":"S","c2":"S","p02ps":1,"y2":"SSSS","n02g":0,"oc":"VV","units":[[0,256,0,2],[0,256,2,4],[256,512,0,2],[256,512,2,4]],"w1first":0,"ost":[[0,2],[2,4]],"wst":[[0,2],[2,4]],"oq":[[0,1,"S"],[1,2,"S"],[2,3,"S"],[3,4,"V"]]}
+
+
+def tile_picked_yafm_none_po_kernel(
+    tc, x_words, x_scales, e_words, e_scales, d_words, d_scales, w1, w2, w3, att, offs, item, cxt, out_0, out_1, out_2
+):
+    nc = tc.nc
+    with ExitStack() as ctx:
+        keep = ctx.enter_context(tc.tile_pool(name="keep", bufs=1))
+        psum = ctx.enter_context(tc.psum_pool(name="psum", bufs=8))
+
+        def sb(shape, dtype, name):
+            return keep.tile(shape, dtype, name=name, align_bytes=64)
+
+        def bank(shape, name):
+            return psum.tile(shape, F32, name=name, tag="bank")
+
+        def load_list(src, name):
+            t = keep.tile([P, S // 16], U16, name=name)
+            nc.sync.dma_start(t[:], src)
+            return t
+
+        def clear_scales(src, name):
+            t = sb([P, src.shape[2]], U8, name)
+            nc.vector.memset(t[:].bitcast(I32), 0)
+            return t
+
+        def load_scales(t, src, row0):
+            for q in range(4):
+                nc.sync.dma_start(t[32 * q + row0 : 32 * q + row0 + 4, :].bitcast(I32), src[0, 4 * q : 4 * q + 4, :].bitcast(I32))
+
+        def load_words(src, name):
+            t = sb([P, src.shape[2]], I32, name)
+            nc.sync.dma_start(t[:], src[0].rearrange("p n t -> p (n t)").bitcast(I32))
+            return t
+
+        def load_weight(src, name):
+            t = sb([P, PACK, N], F32, name)
+            nc.sync.dma_start(t[:], src.rearrange("(p j) c -> p j c", j=PACK))
+            return t
+
+        def quantise_weight(raw, name, engines):
+            g = sb([P, PACK * N], BF16, name + "_g")
+            codes = sb([P, N], U32, name + "_codes")
+            scales = sb([P, N], U8, name + "_scales")
+            dst = g[:].rearrange("p (t m j) -> p m j t", t=PACK, j=PACK)
+            src = raw[:].rearrange("p j (m t) -> p m j t", t=PACK)
+            share = P // len(engines)
+            for i, engine in enumerate(engines):
+                m = slice(i * share, (i + 1) * share)
+                if engine == "S":
+                    nc.scalar.copy(dst[:, m], src[:, m])
+                elif engine == "V":
+                    nc.vector.tensor_copy(dst[:, m], src[:, m])
+                else:
+                    nc.gpsimd.tensor_scalar(dst[:, m], src[:, m], 1.0, 0.0, MULT, ADD)
+            nc.vector.quantize_mx(out=codes[:].bitcast(FP8X4), scales=scales[:], in_=g[:])
+            return codes, scales
+
+        def gather(dst, window, lst, cols):
+            nc.vector.tensor_copy(dst[:, cols], window.indirect(lst[:, cols.start // 16 : cols.stop // 16]))
+
+        def project(out, w, t, words, scales, row0, cols):
+            m = slice(t * P, (t + 1) * P)
+            nc.tensor.matmul_mx(
+                out=out, lhsT=w[0][:, m].bitcast(FP8X4), lhsT_scale=w[1][:, m],
+                rhs=words[:, cols].bitcast(FP8X4), rhs_scale=scales[row0:P, cols], start=True, stop=True,
+            )
+
+        whole = slice(0, S)
+        ds_t = clear_scales(d_scales, "ds_t")
+        xs_t = clear_scales(x_scales, "xs_t")
+        es_t = clear_scales(e_scales, "es_t")
+        cxt_t = load_list(cxt, "cxt_t")
+        offs_t = load_list(offs, "offs_t")
+        load_scales(ds_t, d_scales, 4)
+        w3_raw = load_weight(w3, "w3_raw")
+        load_scales(xs_t, x_scales, 0)
+        w1_raw = load_weight(w1, "w1_raw")
+        dw_t = load_words(d_words, "dw_t")
+        item_t = load_list(item, "item_t")
+        load_scales(es_t, e_scales, 8)
+        xw_t = load_words(x_words, "xw_t")
+        w2_raw = load_weight(w2, "w2_raw")
+        ew_t = load_words(e_words, "ew_t")
+        att_t = sb([P, PACK], F32, "att_t")
+        nc.gpsimd.dma_start(att_t[:], att.rearrange("(p t) o -> p (t o)", t=PACK))
+
+        ident = sb([P, P], F32, "ident")
+        make_identity(nc, ident[:])
+
+        xg_w = sb([P, S], U32, "xg_w")
+        xg_s = sb([P, S], U8, "xg_s")
+        dg_w = sb([P, S], U32, "dg_w")
+        dg_s = sb([P, S], U8, "dg_s")
+        eg_w = sb([P, S], U32, "eg_w")
+        eg_s = sb([P, S], U8, "eg_s")
+
+        ys = sb([P, 2, PACK, S], F32, "ys")
+        p02 = sb([P, PACK, S], F32, "p02")
+        th02 = sb([P, PACK, S], F32, "th02")
+        e02 = sb([P, PACK, S], F32, "e02")
+        n02 = sb([P, PACK, S], F32, "n02")
+
+        gather(dg_s, ds_t[:], cxt_t, whole)
+        w3_q = quantise_weight(w3_raw, "w3", OPT["c3"])
+        gather(dg_w, dw_t[:].bitcast(U32), cxt_t, whole)
+        gather(xg_s, xs_t[:], offs_t, whole)
+        w1_q = quantise_weight(w1_raw, "w1", OPT["c1"])
+        gather(xg_w, xw_t[:].bitcast(U32), offs_t, whole)
+        for t in range(PACK):
+            y = bank([P, S], "y2")
+            project(y[:], w3_q, t, dg_w, dg_s, 4, whole)
+            nc.scalar.copy(ys[:, 1, t, :], y[:])
+        gather(eg_s, es_t[:], item_t, whole)
+        w2_q = quantise_weight(w2_raw, "w2", OPT["c2"])
+        for h in range(2):
+            gather(eg_w, ew_t[:].bitcast(U32), item_t, slice(h * HALF, (h + 1) * HALF))
+        for t in range(PACK):
+            y = bank([P, S], "y0")
+            project(y[:], w1_q, t, xg_w, xg_s, 0, whole)
+            if OPT["p02ps"]:
+                nc.vector.tensor_tensor(p02[:, t, :], ys[:, 1, t, :], y[:], MULT)
+            if OPT["y2"][t] == "S":
+                nc.scalar.copy(ys[:, 0, t, :], y[:])
+            else:
+                nc.vector.tensor_copy(ys[:, 0, t, :], y[:])
+            if not OPT["p02ps"]:
+                nc.vector.tensor_tensor(p02[:, t, :], ys[:, 0, t, :], ys[:, 1, t, :], MULT)
+
+        units = OPT["units"]
+        nu = len(units)
+        wid = [c1 - c0 for (c0, c1, t0, t1) in units]
+        nt = [t1 - t0 for (c0, c1, t0, t1) in units]
+        pp = [sb([P, 2, nt[u], wid[u]], F32, "pp%d" % u) for u in range(nu)]
+        recip = sb([P, 4, PACK * P], F32, "recip")
+        th = [sb([P, 2, nt[u], wid[u]], F32, "th%d" % u)[:] for u in range(nu - 1)]
+        th.append(recip[:, :, 0 : wid[-1]].rearrange("p (k i) w -> p k i w", k=2))
+        ee = [sb([P, 2, nt[u], wid[u]], F32, "ee%d" % u) for u in range(nu)]
+        nn = [sb([P, 2, nt[u], wid[u]], F32, "nn%d" % u) for u in range(nu)]
+        part = sb([P, PACK, S], F32, "part")
+        num = sb([P, PACK, S], F32, "num")
+        dsq = [sb([P, nt[u] * wid[u] // P, P], F32, "dsq%d" % u) for u in range(nu)]
+        back = {}
+
+        def first_pair(u):
+            c0, c1, t0, t1 = units[u]
+            for t in range(t0, t1):
+                nc.scalar.activation(th02[:, t, c0:c1], p02[:, t, c0:c1], ACT.Tanh, scale=att_t[:, t : t + 1])
+            nc.scalar.activation(e02[:, t0:t1, c0:c1], th02[:, t0:t1, c0:c1], ACT.Exp)
+            eng = nc.gpsimd if OPT["n02g"] else nc.vector
+            eng.tensor_tensor(n02[:, t0:t1, c0:c1], p02[:, t0:t1, c0:c1], e02[:, t0:t1, c0:c1], MULT)
+
+        def first_pair_t(tp):
+            for t in range(2 * tp, 2 * tp + 2):
+                nc.scalar.activation(th02[:, t, :], p02[:, t, :], ACT.Tanh, scale=att_t[:, t : t + 1])
+            ts = slice(2 * tp, 2 * tp + 2)
+            nc.scalar.activation(e02[:, ts, :], th02[:, ts, :], ACT.Exp)
+            eng = nc.gpsimd if OPT["n02g"] else nc.vector
+            eng.tensor_tensor(n02[:, ts, :], p02[:, ts, :], e02[:, ts, :], MULT)
+
+        def products(u):
+            c0, c1, t0, t1 = units[u]
+            y = bank([P, nt[u], wid[u]], "y1")
+            for i in range(nt[u]):
+                project(y[:, i, :], w2_q, t0 + i, eg_w, eg_s, 8, slice(c0, c1))
+            nc.vector.tensor_tensor(
+                pp[u][:], ys[:, :, t0:t1, c0:c1], y[:].unsqueeze(1).to_broadcast([P, 2, nt[u], wid[u]]), MULT
+            )
+
+        def weights(u):
+            c0, c1, t0, t1 = units[u]
+            for i in range(nt[u]):
+                t = t0 + i
+                nc.scalar.activation(th[u][:, :, i, :], pp[u][:, :, i, :], ACT.Tanh, scale=att_t[:, t : t + 1])
+            nc.scalar.activation(ee[u][:], th[u], ACT.Exp)
+
+        def numerator(u):
+            c0, c1, t0, t1 = units[u]
+            nc.vector.tensor_tensor(nn[u][:], pp[u][:], ee[u][:], MULT)
+
+        def numerator_a(u):
+            c0, c1, t0, t1 = units[u]
+            nc.vector.tensor_tensor(part[:, t0:t1, c0:c1], nn[u][:, 0], n02[:, t0:t1, c0:c1], ADD)
+
+        def numerator_b(u):
+            c0, c1, t0, t1 = units[u]
+            nc.vector.tensor_tensor(num[:, t0:t1, c0:c1], part[:, t0:t1, c0:c1], nn[u][:, 1], ADD)
+
+        def denominator(u):
+            c0, c1, t0, t1 = units[u]
+            nb = wid[u] // P
+            den = bank([P, nt[u] * nb, P], "den")
+            for i in range(nt[u]):
+                for b in range(nb):
+                    terms = (
+                        e02[:, t0 + i, c0 + b * P : c0 + (b + 1) * P],
+                        ee[u][:, 0, i, b * P : (b + 1) * P],
+                        ee[u][:, 1, i, b * P : (b + 1) * P],
+                    )
+                    for k in range(3):
+                        nc.tensor.matmul(den[:, nb * i + b, :], terms[k], ident[:], start=(k == 0), stop=(k == 2), is_transpose=True)
+            nc.scalar.activation(dsq[u][:], den[:], ACT.Square)
+            for b in range(nb):
+                q = c0 // P + b
+                if q not in back:
+                    back[q] = bank([P, PACK, P], "back")
+                for i in range(nt[u]):
+                    nc.tensor.transpose(back[q][:, t0 + i, :], dsq[u][:, nb * i + b, :], ident[:])
+
+        first_pair_t(0)
+        first_pair_t(1)
+        for u in range(nu):
+            products(u)
+        for u in range(nu):
+            weights(u)
+            numerator(u)
+            denominator(u)
+            numerator_a(u)
+            numerator_b(u)
+
+        out_rows = out_0.rearrange("(p t) j -> p t j", t=PACK)
+        out_words = out_1[0].rearrange("p c r -> p (c r)").bitcast(I32)
+        o_codes = sb([P, S], U32, "o_codes")
+        o_scales = sb([P, S], U8, "o_scales")
+        o = sb([P, PACK, S], F32, "o")
+        for q in range(4):
+            cols = slice(q * P, (q + 1) * P)
+            nc.scalar.activation(recip[:, q, :], back[q][:].rearrange("p t c -> p (t c)"), ACT.Abs_reciprocal_sqrt)
+            nc.vector.tensor_tensor(o[:, :, cols], num[:, :, cols], recip[:, q, :].rearrange("p (t c) -> p t c", t=PACK), MULT)
+            for (qa, qb) in OPT["ost"]:
+                if qb == q + 1:
+                    nc.sync.dma_start(out_rows[:, :, qa * P : qb * P], o[:, :, qa * P : qb * P])
+            for (qa, qb, eng) in OPT["oq"]:
+                if qb == q + 1:
+                    span = slice(qa * P, qb * P)
+                    ob = sb([P, (qb - qa) * P * PACK], BF16, "ob%d" % qa)
+                    dst = ob[:].rearrange("p (c i t) -> p c t i", i=4, t=PACK)
+                    src = o[:, :, span].rearrange("p t (c i) -> p c t i", i=4)
+                    if eng == "S":
+                        nc.scalar.copy(dst, src)
+                    else:
+                        nc.vector.tensor_copy(dst, src)
+                    nc.vector.quantize_mx(out=o_codes[:, span].bitcast(FP8X4), scales=o_scales[:, span], in_=ob[:])
+            for (qa, qb) in OPT["wst"]:
+                if qb == q + 1:
+                    nc.sync.dma_start(out_words[:, qa * P : qb * P], o_codes[:, qa * P : qb * P].bitcast(I32))
+        for q in range(4):
+            (nc.scalar if q % 2 else nc.sync).dma_start(out_2[0, 4 * q : 4 * q + 4, :].bitcast(I32), o_scales[32 * q : 32 * q + 4, :].bitcast(I32))

@@ -21,7 +21,7 @@ N = 512
 S = 512
 HALF = S // 2
 FLOPS = 3 * 2 * K * N * S
-OPT = {"c1":"S","c3":"S","c2":"S","p02ps":1,"y2":"SSSS","n02g":0,"oc":"VV","units":[[0,256,0,2],[0,256,2,4],[256,512,0,2],[256,512,2,4]],"w1first":0,"ost":[[0,2],[2,4]],"wst":[[0,2],[2,4]],"oq":[[0,1,"S"],[1,2,"S"],[2,3,"S"],[3,4,"V"]]}
+OPT = {"c1":"V","c3":"S","c2":"V","p02ps":1,"y2":"SSSS","n02g":0,"oc":"SSSV","units":[[0,256,0,2],[0,256,2,4],[256,512,0,2],[256,512,2,4]],"w1first":0,"ost":[[0,2],[2,4]],"wst":[[0,2],[2,4]],"oq":[[0,1,"V"],[1,2,"S"],[2,3,"S"],[3,4,"V"]],"loads":["cxt","offs","xs","w3","ds","d","w1","x","item","es","w2","e"],"xh":0,"fp":[[0,512,0,2],[0,512,2,4]],"fn":[[0,512,0,2,"V"],[0,512,2,4,"V"]],"esg":0,"alias":0,"wide":1,"esh":0}
 
 
 def tile_picked_yafm_none_po_kernel(
@@ -30,30 +30,30 @@ def tile_picked_yafm_none_po_kernel(
     nc = tc.nc
     with ExitStack() as ctx:
         keep = ctx.enter_context(tc.tile_pool(name="keep", bufs=1))
-        psum = ctx.enter_context(tc.psum_pool(name="psum", bufs=8))
+        psum = ctx.enter_context(tc.psum_pool(name="psum", bufs=1))
 
         def sb(shape, dtype, name):
             return keep.tile(shape, dtype, name=name, align_bytes=64)
 
-        def bank(shape, name):
-            return psum.tile(shape, F32, name=name, tag="bank")
+        def bank(shape, name, tag):
+            return psum.tile(shape, F32, name=name, tag=tag)
 
         def load_list(src, name):
             t = keep.tile([P, S // 16], U16, name=name)
             nc.sync.dma_start(t[:], src)
             return t
 
-        def clear_scales(src, name):
-            t = sb([P, src.shape[2]], U8, name)
-            nc.vector.memset(t[:].bitcast(I32), 0)
+        def clear_scales(src, name, engine):
+            t = keep.tile([P, src.shape[2]], U8, name=name, tag=name, align_bytes=64)
+            engine.memset(t[:].bitcast(I32), 0)
             return t
 
-        def load_scales(t, src, row0):
-            for q in range(4):
-                nc.sync.dma_start(t[32 * q + row0 : 32 * q + row0 + 4, :].bitcast(I32), src[0, 4 * q : 4 * q + 4, :].bitcast(I32))
+        def load_scales(queue, t, src, row0):
+            for r in range(4):
+                queue.dma_start(t[row0 + r : P : 32, :].bitcast(I32), src[0, r:16:4, :].bitcast(I32))
 
         def load_words(src, name):
-            t = sb([P, src.shape[2]], I32, name)
+            t = keep.tile([P, src.shape[2]], I32, name=name, tag=name, align_bytes=64)
             nc.sync.dma_start(t[:], src[0].rearrange("p n t -> p (n t)").bitcast(I32))
             return t
 
@@ -91,74 +91,104 @@ def tile_picked_yafm_none_po_kernel(
             )
 
         whole = slice(0, S)
-        ds_t = clear_scales(d_scales, "ds_t")
-        xs_t = clear_scales(x_scales, "xs_t")
-        es_t = clear_scales(e_scales, "es_t")
-        cxt_t = load_list(cxt, "cxt_t")
-        offs_t = load_list(offs, "offs_t")
-        load_scales(ds_t, d_scales, 4)
-        w3_raw = load_weight(w3, "w3_raw")
-        load_scales(xs_t, x_scales, 0)
-        w1_raw = load_weight(w1, "w1_raw")
-        dw_t = load_words(d_words, "dw_t")
-        item_t = load_list(item, "item_t")
-        load_scales(es_t, e_scales, 8)
-        xw_t = load_words(x_words, "xw_t")
-        w2_raw = load_weight(w2, "w2_raw")
-        ew_t = load_words(e_words, "ew_t")
+        xs_t = clear_scales(x_scales, "xs_t", nc.gpsimd)
+        ds_t = clear_scales(d_scales, "ds_t", nc.vector)
+        es_t = clear_scales(e_scales, "es_t", nc.vector)
+        T = {}
+        for nm in OPT["loads"]:
+            if nm == "cxt":
+                cxt_t = load_list(cxt, "cxt_t")
+            elif nm == "offs":
+                offs_t = load_list(offs, "offs_t")
+            elif nm == "item":
+                item_t = load_list(item, "item_t")
+            elif nm == "ds":
+                load_scales(nc.sync, ds_t, d_scales, 4)
+            elif nm == "xs":
+                load_scales(nc.sync, xs_t, x_scales, 0)
+            elif nm == "es":
+                load_scales(nc.gpsimd if OPT["esg"] else nc.sync, es_t, e_scales, 8)
+            elif nm == "w1":
+                w1_raw = load_weight(w1, "w1_raw")
+            elif nm == "w2":
+                w2_raw = load_weight(w2, "w2_raw")
+            elif nm == "w3":
+                w3_raw = load_weight(w3, "w3_raw")
+            elif nm == "x":
+                xw_t = load_words(x_words, "xw_t")
+            elif nm == "d":
+                dw_t = load_words(d_words, "dw_t")
+            elif nm == "e":
+                ew_t = load_words(e_words, "ew_t")
         att_t = sb([P, PACK], F32, "att_t")
         nc.gpsimd.dma_start(att_t[:], att.rearrange("(p t) o -> p (t o)", t=PACK))
 
         ident = sb([P, P], F32, "ident")
         make_identity(nc, ident[:])
 
-        xg_w = sb([P, S], U32, "xg_w")
         xg_s = sb([P, S], U8, "xg_s")
         dg_w = sb([P, S], U32, "dg_w")
         dg_s = sb([P, S], U8, "dg_s")
         eg_w = sb([P, S], U32, "eg_w")
         eg_s = sb([P, S], U8, "eg_s")
 
-        ys = sb([P, 2, PACK, S], F32, "ys")
+        ys = sb([P, PACK, 2, S], F32, "ys")
         p02 = sb([P, PACK, S], F32, "p02")
         th02 = sb([P, PACK, S], F32, "th02")
         e02 = sb([P, PACK, S], F32, "e02")
-        n02 = sb([P, PACK, S], F32, "n02")
 
+        halves = [slice(h * HALF, (h + 1) * HALF) for h in range(2)]
         gather(dg_s, ds_t[:], cxt_t, whole)
         w3_q = quantise_weight(w3_raw, "w3", OPT["c3"])
-        gather(dg_w, dw_t[:].bitcast(U32), cxt_t, whole)
         gather(xg_s, xs_t[:], offs_t, whole)
         w1_q = quantise_weight(w1_raw, "w1", OPT["c1"])
-        gather(xg_w, xw_t[:].bitcast(U32), offs_t, whole)
+        gather(dg_w, dw_t[:].bitcast(U32), cxt_t, whole)
+        if OPT["alias"]:
+            gather(eg_s, es_t[:], item_t, whole)
+            xg_w = keep.tile([P, S], U32, name="xg_w", tag="es_t", align_bytes=64)
+        else:
+            xg_w = sb([P, S], U32, "xg_w")
+        if OPT["xh"]:
+            for cols in halves:
+                gather(xg_w, xw_t[:].bitcast(U32), offs_t, cols)
+        else:
+            gather(xg_w, xw_t[:].bitcast(U32), offs_t, whole)
         for t in range(PACK):
-            y = bank([P, S], "y2")
+            y = bank([P, S], "y2", "a%d" % t)
             project(y[:], w3_q, t, dg_w, dg_s, 4, whole)
-            nc.scalar.copy(ys[:, 1, t, :], y[:])
-        gather(eg_s, es_t[:], item_t, whole)
+            nc.scalar.copy(ys[:, t, 1, :], y[:])
+        if not OPT["alias"]:
+            gather(eg_s, es_t[:], item_t, whole)
         w2_q = quantise_weight(w2_raw, "w2", OPT["c2"])
-        for h in range(2):
-            gather(eg_w, ew_t[:].bitcast(U32), item_t, slice(h * HALF, (h + 1) * HALF))
-        for t in range(PACK):
-            y = bank([P, S], "y0")
-            project(y[:], w1_q, t, xg_w, xg_s, 0, whole)
+        for cols in halves:
+            gather(eg_w, ew_t[:].bitcast(U32), item_t, cols)
+        if OPT["xh"]:
+            pieces = [(cols, slice(2 * tp, 2 * tp + 2)) for cols in halves for tp in range(2)]
+        else:
+            pieces = [(whole, slice(t, t + 1)) for t in range(PACK)]
+        for k, (cols, ts) in enumerate(pieces):
+            y = bank([P, ts.stop - ts.start, cols.stop - cols.start], "y0", "a%d" % k)
+            for t in range(ts.start, ts.stop):
+                project(y[:, t - ts.start, :], w1_q, t, xg_w, xg_s, 0, cols)
             if OPT["p02ps"]:
-                nc.vector.tensor_tensor(p02[:, t, :], ys[:, 1, t, :], y[:], MULT)
-            if OPT["y2"][t] == "S":
-                nc.scalar.copy(ys[:, 0, t, :], y[:])
+                nc.vector.tensor_tensor(p02[:, ts, cols], ys[:, ts, 1, cols], y[:], MULT)
+            if OPT["y2"][k] == "S":
+                nc.scalar.copy(ys[:, ts, 0, cols], y[:])
             else:
-                nc.vector.tensor_copy(ys[:, 0, t, :], y[:])
+                nc.vector.tensor_copy(ys[:, ts, 0, cols], y[:])
             if not OPT["p02ps"]:
-                nc.vector.tensor_tensor(p02[:, t, :], ys[:, 0, t, :], ys[:, 1, t, :], MULT)
+                nc.vector.tensor_tensor(p02[:, ts, cols], ys[:, ts, 0, cols], ys[:, ts, 1, cols], MULT)
 
+        n02 = keep.tile([P, PACK, S], F32, name="n02", tag="ew_t", align_bytes=64)
         units = OPT["units"]
         nu = len(units)
         wid = [c1 - c0 for (c0, c1, t0, t1) in units]
         nt = [t1 - t0 for (c0, c1, t0, t1) in units]
         pp = [sb([P, 2, nt[u], wid[u]], F32, "pp%d" % u) for u in range(nu)]
-        recip = sb([P, 4, PACK * P], F32, "recip")
-        th = [sb([P, 2, nt[u], wid[u]], F32, "th%d" % u)[:] for u in range(nu - 1)]
-        th.append(recip[:, :, 0 : wid[-1]].rearrange("p (k i) w -> p k i w", k=2))
+        recip = sb([P, PACK, S], F32, "recip")
+        run = [nt[u] * wid[u] // PACK for u in range(nu)]
+        th = [sb([P, 2, PACK, run[u]], F32, "th%d" % u)[:] for u in range(nu - 1)]
+        th.append(recip[:].rearrange("p t (h w) -> p h t w", h=2)[:, :, :, 0 : run[-1]])
         ee = [sb([P, 2, nt[u], wid[u]], F32, "ee%d" % u) for u in range(nu)]
         nn = [sb([P, 2, nt[u], wid[u]], F32, "nn%d" % u) for u in range(nu)]
         part = sb([P, PACK, S], F32, "part")
@@ -166,37 +196,32 @@ def tile_picked_yafm_none_po_kernel(
         dsq = [sb([P, nt[u] * wid[u] // P, P], F32, "dsq%d" % u) for u in range(nu)]
         back = {}
 
-        def first_pair(u):
-            c0, c1, t0, t1 = units[u]
-            for t in range(t0, t1):
-                nc.scalar.activation(th02[:, t, c0:c1], p02[:, t, c0:c1], ACT.Tanh, scale=att_t[:, t : t + 1])
-            nc.scalar.activation(e02[:, t0:t1, c0:c1], th02[:, t0:t1, c0:c1], ACT.Exp)
-            eng = nc.gpsimd if OPT["n02g"] else nc.vector
-            eng.tensor_tensor(n02[:, t0:t1, c0:c1], p02[:, t0:t1, c0:c1], e02[:, t0:t1, c0:c1], MULT)
+        def first_pair(cols, ts):
+            for t in range(ts.start, ts.stop):
+                nc.scalar.activation(th02[:, t, cols], p02[:, t, cols], ACT.Tanh, scale=att_t[:, t : t + 1])
+            nc.scalar.activation(e02[:, ts, cols], th02[:, ts, cols], ACT.Exp)
 
-        def first_pair_t(tp):
-            for t in range(2 * tp, 2 * tp + 2):
-                nc.scalar.activation(th02[:, t, :], p02[:, t, :], ACT.Tanh, scale=att_t[:, t : t + 1])
-            ts = slice(2 * tp, 2 * tp + 2)
-            nc.scalar.activation(e02[:, ts, :], th02[:, ts, :], ACT.Exp)
-            eng = nc.gpsimd if OPT["n02g"] else nc.vector
-            eng.tensor_tensor(n02[:, ts, :], p02[:, ts, :], e02[:, ts, :], MULT)
+        def first_num(cols, ts, eng):
+            (nc.gpsimd if eng == "G" else nc.vector).tensor_tensor(n02[:, ts, cols], p02[:, ts, cols], e02[:, ts, cols], MULT)
 
         def products(u):
             c0, c1, t0, t1 = units[u]
-            y = bank([P, nt[u], wid[u]], "y1")
+            y = bank([P, nt[u], wid[u]], "y1", btag[u])
             for i in range(nt[u]):
                 project(y[:, i, :], w2_q, t0 + i, eg_w, eg_s, 8, slice(c0, c1))
             nc.vector.tensor_tensor(
-                pp[u][:], ys[:, :, t0:t1, c0:c1], y[:].unsqueeze(1).to_broadcast([P, 2, nt[u], wid[u]]), MULT
+                pp[u][:], ys[:, t0:t1, :, c0:c1].rearrange("p t k c -> p k t c"), y[:].unsqueeze(1).to_broadcast([P, 2, nt[u], wid[u]]), MULT
             )
 
         def weights(u):
             c0, c1, t0, t1 = units[u]
             for i in range(nt[u]):
                 t = t0 + i
-                nc.scalar.activation(th[u][:, :, i, :], pp[u][:, :, i, :], ACT.Tanh, scale=att_t[:, t : t + 1])
-            nc.scalar.activation(ee[u][:], th[u], ACT.Exp)
+                k = PACK // nt[u]
+                nc.scalar.activation(
+                    th[u][:, :, i * k : (i + 1) * k, :], pp[u][:, :, i, :].rearrange("p h (k w) -> p h k w", k=k), ACT.Tanh, scale=att_t[:, t : t + 1]
+                )
+            nc.scalar.activation(ee[u][:].rearrange("p h i (k w) -> p h (i k) w", w=run[u]), th[u], ACT.Exp)
 
         def numerator(u):
             c0, c1, t0, t1 = units[u]
@@ -210,31 +235,46 @@ def tile_picked_yafm_none_po_kernel(
             c0, c1, t0, t1 = units[u]
             nc.vector.tensor_tensor(num[:, t0:t1, c0:c1], part[:, t0:t1, c0:c1], nn[u][:, 1], ADD)
 
+        den = {}
+        btag = ["b0", "b1", "b2", "b3", "a0"]
+
+        def blocks(u):
+            c0, c1, t0, t1 = units[u]
+            return [(i, b) for i in range(nt[u]) for b in range(wid[u] // P)]
+
+        def den_open(u):
+            c0, c1, t0, t1 = units[u]
+            den[u] = bank([P, len(blocks(u)), P], "den", btag[u])
+            for k, (i, b) in enumerate(blocks(u)):
+                nc.tensor.matmul(den[u][:, k, :], e02[:, t0 + i, c0 + b * P : c0 + (b + 1) * P], ident[:], start=(k == 0), stop=False, is_transpose=True)
+
         def denominator(u):
             c0, c1, t0, t1 = units[u]
-            nb = wid[u] // P
-            den = bank([P, nt[u] * nb, P], "den")
-            for i in range(nt[u]):
-                for b in range(nb):
-                    terms = (
-                        e02[:, t0 + i, c0 + b * P : c0 + (b + 1) * P],
-                        ee[u][:, 0, i, b * P : (b + 1) * P],
-                        ee[u][:, 1, i, b * P : (b + 1) * P],
-                    )
-                    for k in range(3):
-                        nc.tensor.matmul(den[:, nb * i + b, :], terms[k], ident[:], start=(k == 0), stop=(k == 2), is_transpose=True)
-            nc.scalar.activation(dsq[u][:], den[:], ACT.Square)
-            for b in range(nb):
-                q = c0 // P + b
-                if q not in back:
-                    back[q] = bank([P, PACK, P], "back")
-                for i in range(nt[u]):
-                    nc.tensor.transpose(back[q][:, t0 + i, :], dsq[u][:, nb * i + b, :], ident[:])
+            last = len(blocks(u)) - 1
+            if OPT["wide"]:
+                for pair in range(2):
+                    for k, (i, b) in enumerate(blocks(u)):
+                        nc.tensor.matmul(den[u][:, k, :], ee[u][:, pair, i, b * P : (b + 1) * P], ident[:], start=False, stop=(pair == 1 and k == last), is_transpose=True)
+            else:
+                den[u] = bank([P, len(blocks(u)), P], "den", btag[u])
+                for k, (i, b) in enumerate(blocks(u)):
+                    terms = (e02[:, t0 + i, c0 + b * P : c0 + (b + 1) * P], ee[u][:, 0, i, b * P : (b + 1) * P], ee[u][:, 1, i, b * P : (b + 1) * P])
+                    for j in range(3):
+                        nc.tensor.matmul(den[u][:, k, :], terms[j], ident[:], start=(j == 0), stop=(j == 2), is_transpose=True)
+            nc.scalar.activation(dsq[u][:], den[u][:], ACT.Square)
+            back[u] = bank([P, last + 1, P], "back", btag[u])
+            for k in range(last + 1):
+                nc.tensor.transpose(back[u][:, k, :], dsq[u][:, k, :], ident[:])
 
-        first_pair_t(0)
-        first_pair_t(1)
+        for (c0, c1, t0, t1) in OPT["fp"]:
+            first_pair(slice(c0, c1), slice(t0, t1))
         for u in range(nu):
             products(u)
+        if OPT["wide"]:
+            for u in range(nu):
+                den_open(u)
+        for (c0, c1, t0, t1, eng) in OPT["fn"]:
+            first_num(slice(c0, c1), slice(t0, t1), eng)
         for u in range(nu):
             weights(u)
             numerator(u)
@@ -246,27 +286,25 @@ def tile_picked_yafm_none_po_kernel(
         out_words = out_1[0].rearrange("p c r -> p (c r)").bitcast(I32)
         o_codes = sb([P, S], U32, "o_codes")
         o_scales = sb([P, S], U8, "o_scales")
-        o = sb([P, PACK, S], F32, "o")
+        o = [sb([P, PACK, HALF], F32, "o%d" % h) for h in range(2)]
+        for u in range(nu):
+            c0, c1, t0, t1 = units[u]
+            h = c0 // HALF
+            nc.scalar.activation(recip[:, t0:t1, c0:c1], back[u][:].rearrange("p (i b) c -> p i (b c)", i=nt[u]), ACT.Abs_reciprocal_sqrt)
+            nc.vector.tensor_tensor(o[h][:, t0:t1, :], num[:, t0:t1, c0:c1], recip[:, t0:t1, c0:c1], MULT)
+            if t1 == PACK:
+                nc.sync.dma_start(out_rows[:, :, halves[h]], o[h][:])
+        ob = [sb([P, HALF * PACK], BF16, "ob%d" % h) for h in range(2)]
         for q in range(4):
-            cols = slice(q * P, (q + 1) * P)
-            nc.scalar.activation(recip[:, q, :], back[q][:].rearrange("p t c -> p (t c)"), ACT.Abs_reciprocal_sqrt)
-            nc.vector.tensor_tensor(o[:, :, cols], num[:, :, cols], recip[:, q, :].rearrange("p (t c) -> p t c", t=PACK), MULT)
-            for (qa, qb) in OPT["ost"]:
-                if qb == q + 1:
-                    nc.sync.dma_start(out_rows[:, :, qa * P : qb * P], o[:, :, qa * P : qb * P])
-            for (qa, qb, eng) in OPT["oq"]:
-                if qb == q + 1:
-                    span = slice(qa * P, qb * P)
-                    ob = sb([P, (qb - qa) * P * PACK], BF16, "ob%d" % qa)
-                    dst = ob[:].rearrange("p (c i t) -> p c t i", i=4, t=PACK)
-                    src = o[:, :, span].rearrange("p t (c i) -> p c t i", i=4)
-                    if eng == "S":
-                        nc.scalar.copy(dst, src)
-                    else:
-                        nc.vector.tensor_copy(dst, src)
-                    nc.vector.quantize_mx(out=o_codes[:, span].bitcast(FP8X4), scales=o_scales[:, span], in_=ob[:])
-            for (qa, qb) in OPT["wst"]:
-                if qb == q + 1:
-                    nc.sync.dma_start(out_words[:, qa * P : qb * P], o_codes[:, qa * P : qb * P].bitcast(I32))
+            h, r = divmod(q, 2)
+            dst = ob[h][:, r * P * PACK : (r + 1) * P * PACK].rearrange("p (c i t) -> p c t i", i=4, t=PACK)
+            src = o[h][:, :, r * P : (r + 1) * P].rearrange("p t (c i) -> p c t i", i=4)
+            if OPT["oc"][q] == "S":
+                nc.scalar.copy(dst, src)
+            else:
+                nc.vector.tensor_copy(dst, src)
+            if r == 1:
+                nc.vector.quantize_mx(out=o_codes[:, halves[h]].bitcast(FP8X4), scales=o_scales[:, halves[h]], in_=ob[h][:])
+                nc.sync.dma_start(out_words[:, halves[h]], o_codes[:, halves[h]].bitcast(I32))
         for q in range(4):
-            (nc.scalar if q % 2 else nc.sync).dma_start(out_2[0, 4 * q : 4 * q + 4, :].bitcast(I32), o_scales[32 * q : 32 * q + 4, :].bitcast(I32))
+            (nc.scalar if q % 2 else nc.sync).dma_start(out_2[0, q:16:4, :].bitcast(I32), o_scales[q:P:32, :].bitcast(I32))

@@ -20,291 +20,217 @@ K = 512
 N = 512
 S = 512
 HALF = S // 2
+QUAD = 32
+LIST_ROWS = 16
+X_ROW, D_ROW, E_ROW = 0, 4, 8
 FLOPS = 3 * 2 * K * N * S
-OPT = {"c1":"V","c3":"S","c2":"V","p02ps":1,"y2":"SSSS","n02g":0,"oc":"SSSV","units":[[0,256,0,2],[0,256,2,4],[256,512,0,2],[256,512,2,4]],"w1first":0,"ost":[[0,2],[2,4]],"wst":[[0,2],[2,4]],"oq":[[0,1,"V"],[1,2,"S"],[2,3,"S"],[3,4,"V"]],"loads":["cxt","offs","xs","w3","ds","d","w1","x","item","es","w2","e"],"xh":0,"fp":[[0,512,0,2],[0,512,2,4]],"fn":[[0,512,0,2,"V"],[0,512,2,4,"V"]],"esg":0,"alias":0,"wide":1,"esh":0}
 
 
 def tile_picked_yafm_none_po_kernel(
     tc, x_words, x_scales, e_words, e_scales, d_words, d_scales, w1, w2, w3, att, offs, item, cxt, out_0, out_1, out_2
 ):
     nc = tc.nc
+    whole = slice(0, S)
+    halves = [slice(h * HALF, (h + 1) * HALF) for h in range(2)]
+    duos = [slice(2 * d, 2 * d + 2) for d in range(2)]
+    units = [(cols, duo) for cols in halves for duo in duos]
+    blocks = [(i, c) for i in range(2) for c in range(0, HALF, P)]
+
     with ExitStack() as ctx:
         keep = ctx.enter_context(tc.tile_pool(name="keep", bufs=1))
         psum = ctx.enter_context(tc.psum_pool(name="psum", bufs=1))
 
-        def sb(shape, dtype, name):
-            return keep.tile(shape, dtype, name=name, align_bytes=64)
-
-        def bank(shape, name, tag):
-            return psum.tile(shape, F32, name=name, tag=tag)
+        def sb(shape, dtype, name, tag=None):
+            return keep.tile(shape, dtype, name=name, tag=tag or name, align_bytes=64)
 
         def load_list(src, name):
-            t = keep.tile([P, S // 16], U16, name=name)
-            nc.sync.dma_start(t[:], src)
-            return t
+            tile = keep.tile([P, S // LIST_ROWS], U16, name=name)
+            nc.sync.dma_start(tile[:], src)
+            return tile
 
-        def clear_scales(src, name, engine):
-            t = keep.tile([P, src.shape[2]], U8, name=name, tag=name, align_bytes=64)
-            engine.memset(t[:].bitcast(I32), 0)
-            return t
+        def cleared_scales(src, name, engine):
+            tile = sb([P, src.shape[2]], U8, name)
+            engine.memset(tile[:].bitcast(I32), 0)
+            return tile
 
-        def load_scales(queue, t, src, row0):
+        def load_scales(tile, src, row0):
             for r in range(4):
-                queue.dma_start(t[row0 + r : P : 32, :].bitcast(I32), src[0, r:16:4, :].bitcast(I32))
+                nc.sync.dma_start(tile[row0 + r : P : QUAD, :].bitcast(I32), src[0, r:16:4, :].bitcast(I32))
 
         def load_words(src, name):
-            t = keep.tile([P, src.shape[2]], I32, name=name, tag=name, align_bytes=64)
-            nc.sync.dma_start(t[:], src[0].rearrange("p n t -> p (n t)").bitcast(I32))
-            return t
+            tile = sb([P, src.shape[2]], I32, name)
+            nc.sync.dma_start(tile[:], src[0].rearrange("p n t -> p (n t)").bitcast(I32))
+            return tile
 
         def load_weight(src, name):
-            t = sb([P, PACK, N], F32, name)
-            nc.sync.dma_start(t[:], src.rearrange("(p j) c -> p j c", j=PACK))
-            return t
+            tile = sb([P, PACK, N], F32, name)
+            nc.sync.dma_start(tile[:], src.rearrange("(p j) c -> p j c", j=PACK))
+            return tile
 
-        def quantise_weight(raw, name, engines):
-            g = sb([P, PACK * N], BF16, name + "_g")
+        def quantise_weight(raw, name, copy, parts):
             codes = sb([P, N], U32, name + "_codes")
             scales = sb([P, N], U8, name + "_scales")
-            dst = g[:].rearrange("p (t m j) -> p m j t", t=PACK, j=PACK)
-            src = raw[:].rearrange("p j (m t) -> p m j t", t=PACK)
-            share = P // len(engines)
-            for i, engine in enumerate(engines):
-                m = slice(i * share, (i + 1) * share)
-                if engine == "S":
-                    nc.scalar.copy(dst[:, m], src[:, m])
-                elif engine == "V":
-                    nc.vector.tensor_copy(dst[:, m], src[:, m])
-                else:
-                    nc.gpsimd.tensor_scalar(dst[:, m], src[:, m], 1.0, 0.0, MULT, ADD)
-            nc.vector.quantize_mx(out=codes[:].bitcast(FP8X4), scales=scales[:], in_=g[:])
+            share = PACK // parts
+            for i in range(parts):
+                grouped = sb([P, share * N], BF16, name + "_grouped%d" % i)
+                copy(
+                    grouped[:].rearrange("p (t m j) -> p m j t", t=share, j=PACK),
+                    raw[:].rearrange("p j (m t) -> p m j t", t=PACK)[:, :, :, i * share : (i + 1) * share],
+                )
+                span = slice(i * share * P, (i + 1) * share * P)
+                nc.vector.quantize_mx(out=codes[:, span].bitcast(FP8X4), scales=scales[:, span], in_=grouped[:])
             return codes, scales
 
-        def gather(dst, window, lst, cols):
-            nc.vector.tensor_copy(dst[:, cols], window.indirect(lst[:, cols.start // 16 : cols.stop // 16]))
+        def gather(dst, window, entries, cols):
+            nc.vector.tensor_copy(dst[:, cols], window.indirect(entries[:, cols.start // LIST_ROWS : cols.stop // LIST_ROWS]))
 
-        def project(out, w, t, words, scales, row0, cols):
+        def project(out, weight, t, words, scales, row0, cols):
             m = slice(t * P, (t + 1) * P)
             nc.tensor.matmul_mx(
-                out=out, lhsT=w[0][:, m].bitcast(FP8X4), lhsT_scale=w[1][:, m],
+                out=out, lhsT=weight[0][:, m].bitcast(FP8X4), lhsT_scale=weight[1][:, m],
                 rhs=words[:, cols].bitcast(FP8X4), rhs_scale=scales[row0:P, cols], start=True, stop=True,
             )
 
-        whole = slice(0, S)
-        xs_t = clear_scales(x_scales, "xs_t", nc.gpsimd)
-        ds_t = clear_scales(d_scales, "ds_t", nc.vector)
-        es_t = clear_scales(e_scales, "es_t", nc.vector)
-        T = {}
-        for nm in OPT["loads"]:
-            if nm == "cxt":
-                cxt_t = load_list(cxt, "cxt_t")
-            elif nm == "offs":
-                offs_t = load_list(offs, "offs_t")
-            elif nm == "item":
-                item_t = load_list(item, "item_t")
-            elif nm == "ds":
-                load_scales(nc.sync, ds_t, d_scales, 4)
-            elif nm == "xs":
-                load_scales(nc.sync, xs_t, x_scales, 0)
-            elif nm == "es":
-                load_scales(nc.gpsimd if OPT["esg"] else nc.sync, es_t, e_scales, 8)
-            elif nm == "w1":
-                w1_raw = load_weight(w1, "w1_raw")
-            elif nm == "w2":
-                w2_raw = load_weight(w2, "w2_raw")
-            elif nm == "w3":
-                w3_raw = load_weight(w3, "w3_raw")
-            elif nm == "x":
-                xw_t = load_words(x_words, "xw_t")
-            elif nm == "d":
-                dw_t = load_words(d_words, "dw_t")
-            elif nm == "e":
-                ew_t = load_words(e_words, "ew_t")
+        x_scale_table = cleared_scales(x_scales, "x_scale_table", nc.gpsimd)
+        d_scale_table = cleared_scales(d_scales, "d_scale_table", nc.vector)
+        e_scale_table = cleared_scales(e_scales, "e_scale_table", nc.vector)
+        d_list = load_list(cxt, "d_list")
+        x_list = load_list(offs, "x_list")
+        load_scales(x_scale_table, x_scales, X_ROW)
+        w3_raw = load_weight(w3, "w3_raw")
+        load_scales(d_scale_table, d_scales, D_ROW)
+        d_word_table = load_words(d_words, "d_word_table")
+        w1_raw = load_weight(w1, "w1_raw")
+        x_word_table = load_words(x_words, "x_word_table")
+        e_list = load_list(item, "e_list")
+        load_scales(e_scale_table, e_scales, E_ROW)
+        w2_raw = load_weight(w2, "w2_raw")
+        e_word_table = load_words(e_words, "e_word_table")
         att_t = sb([P, PACK], F32, "att_t")
         nc.gpsimd.dma_start(att_t[:], att.rearrange("(p t) o -> p (t o)", t=PACK))
 
         ident = sb([P, P], F32, "ident")
         make_identity(nc, ident[:])
 
-        xg_s = sb([P, S], U8, "xg_s")
-        dg_w = sb([P, S], U32, "dg_w")
-        dg_s = sb([P, S], U8, "dg_s")
-        eg_w = sb([P, S], U32, "eg_w")
-        eg_s = sb([P, S], U8, "eg_s")
+        x_picked_scales = sb([P, S], U8, "x_picked_scales")
+        x_picked_words = sb([P, S], U32, "x_picked_words")
+        d_picked_scales = sb([P, S], U8, "d_picked_scales")
+        d_picked_words = sb([P, S], U32, "d_picked_words")
+        e_picked_scales = sb([P, S], U8, "e_picked_scales")
+        e_picked_words = sb([P, S], U32, "e_picked_words")
 
-        ys = sb([P, PACK, 2, S], F32, "ys")
+        y02 = sb([P, PACK, 2, S], F32, "y02")
         p02 = sb([P, PACK, S], F32, "p02")
-        th02 = sb([P, PACK, S], F32, "th02")
+        tanh02 = sb([P, PACK, S], F32, "tanh02")
         e02 = sb([P, PACK, S], F32, "e02")
 
-        halves = [slice(h * HALF, (h + 1) * HALF) for h in range(2)]
-        gather(dg_s, ds_t[:], cxt_t, whole)
-        w3_q = quantise_weight(w3_raw, "w3", OPT["c3"])
-        gather(xg_s, xs_t[:], offs_t, whole)
-        w1_q = quantise_weight(w1_raw, "w1", OPT["c1"])
-        gather(dg_w, dw_t[:].bitcast(U32), cxt_t, whole)
-        if OPT["alias"]:
-            gather(eg_s, es_t[:], item_t, whole)
-            xg_w = keep.tile([P, S], U32, name="xg_w", tag="es_t", align_bytes=64)
-        else:
-            xg_w = sb([P, S], U32, "xg_w")
-        if OPT["xh"]:
-            for cols in halves:
-                gather(xg_w, xw_t[:].bitcast(U32), offs_t, cols)
-        else:
-            gather(xg_w, xw_t[:].bitcast(U32), offs_t, whole)
+        gather(d_picked_scales, d_scale_table[:], d_list, whole)
+        w3_q = quantise_weight(w3_raw, "w3", nc.scalar.copy, 1)
+        gather(x_picked_scales, x_scale_table[:], x_list, whole)
+        w1_q = quantise_weight(w1_raw, "w1", nc.vector.tensor_copy, 2)
+        gather(d_picked_words, d_word_table[:].bitcast(U32), d_list, whole)
+        gather(x_picked_words, x_word_table[:].bitcast(U32), x_list, whole)
+
         for t in range(PACK):
-            y = bank([P, S], "y2", "a%d" % t)
-            project(y[:], w3_q, t, dg_w, dg_s, 4, whole)
-            nc.scalar.copy(ys[:, t, 1, :], y[:])
-        if not OPT["alias"]:
-            gather(eg_s, es_t[:], item_t, whole)
-        w2_q = quantise_weight(w2_raw, "w2", OPT["c2"])
+            y2 = psum.tile([P, S], F32, name="y2", tag="tile%d" % t)
+            project(y2[:], w3_q, t, d_picked_words, d_picked_scales, D_ROW, whole)
+            nc.scalar.copy(y02[:, t, 1, :], y2[:])
+        y0 = []
+        for t in range(PACK):
+            y0.append(psum.tile([P, S], F32, name="y0", tag="tile%d" % t))
+            project(y0[t][:], w1_q, t, x_picked_words, x_picked_scales, X_ROW, whole)
+            nc.vector.tensor_tensor(p02[:, t, :], y02[:, t, 1, :], y0[t][:], MULT)
+
+        def keep_y0(duo):
+            for t in range(duo.start, duo.stop):
+                nc.scalar.copy(y02[:, t, 0, :], y0[t][:])
+
+        keep_y0(duos[0])
+
+        gather(e_picked_scales, e_scale_table[:], e_list, whole)
+        w2_q = quantise_weight(w2_raw, "w2", nc.vector.tensor_copy, 2)
         for cols in halves:
-            gather(eg_w, ew_t[:].bitcast(U32), item_t, cols)
-        if OPT["xh"]:
-            pieces = [(cols, slice(2 * tp, 2 * tp + 2)) for cols in halves for tp in range(2)]
-        else:
-            pieces = [(whole, slice(t, t + 1)) for t in range(PACK)]
-        for k, (cols, ts) in enumerate(pieces):
-            y = bank([P, ts.stop - ts.start, cols.stop - cols.start], "y0", "a%d" % k)
-            for t in range(ts.start, ts.stop):
-                project(y[:, t - ts.start, :], w1_q, t, xg_w, xg_s, 0, cols)
-            if OPT["p02ps"]:
-                nc.vector.tensor_tensor(p02[:, ts, cols], ys[:, ts, 1, cols], y[:], MULT)
-            if OPT["y2"][k] == "S":
-                nc.scalar.copy(ys[:, ts, 0, cols], y[:])
-            else:
-                nc.vector.tensor_copy(ys[:, ts, 0, cols], y[:])
-            if not OPT["p02ps"]:
-                nc.vector.tensor_tensor(p02[:, ts, cols], ys[:, ts, 0, cols], ys[:, ts, 1, cols], MULT)
+            gather(e_picked_words, e_word_table[:].bitcast(U32), e_list, cols)
 
-        n02 = keep.tile([P, PACK, S], F32, name="n02", tag="ew_t", align_bytes=64)
-        units = OPT["units"]
-        nu = len(units)
-        wid = [c1 - c0 for (c0, c1, t0, t1) in units]
-        nt = [t1 - t0 for (c0, c1, t0, t1) in units]
-        pp = [sb([P, 2, nt[u], wid[u]], F32, "pp%d" % u) for u in range(nu)]
-        recip = sb([P, PACK, S], F32, "recip")
-        run = [nt[u] * wid[u] // PACK for u in range(nu)]
-        th = [sb([P, 2, PACK, run[u]], F32, "th%d" % u)[:] for u in range(nu - 1)]
-        th.append(recip[:].rearrange("p t (h w) -> p h t w", h=2)[:, :, :, 0 : run[-1]])
-        ee = [sb([P, 2, nt[u], wid[u]], F32, "ee%d" % u) for u in range(nu)]
-        nn = [sb([P, 2, nt[u], wid[u]], F32, "nn%d" % u) for u in range(nu)]
-        part = sb([P, PACK, S], F32, "part")
-        num = sb([P, PACK, S], F32, "num")
-        dsq = [sb([P, nt[u] * wid[u] // P, P], F32, "dsq%d" % u) for u in range(nu)]
-        back = {}
+        for duo in duos:
+            for t in range(duo.start, duo.stop):
+                nc.scalar.activation(tanh02[:, t, :], p02[:, t, :], ACT.Tanh, scale=att_t[:, t : t + 1])
+            nc.scalar.activation(e02[:, duo, :], tanh02[:, duo, :], ACT.Exp)
+        keep_y0(duos[1])
 
-        def first_pair(cols, ts):
-            for t in range(ts.start, ts.stop):
-                nc.scalar.activation(th02[:, t, cols], p02[:, t, cols], ACT.Tanh, scale=att_t[:, t : t + 1])
-            nc.scalar.activation(e02[:, ts, cols], th02[:, ts, cols], ACT.Exp)
-
-        def first_num(cols, ts, eng):
-            (nc.gpsimd if eng == "G" else nc.vector).tensor_tensor(n02[:, ts, cols], p02[:, ts, cols], e02[:, ts, cols], MULT)
-
-        def products(u):
-            c0, c1, t0, t1 = units[u]
-            y = bank([P, nt[u], wid[u]], "y1", btag[u])
-            for i in range(nt[u]):
-                project(y[:, i, :], w2_q, t0 + i, eg_w, eg_s, 8, slice(c0, c1))
+        pair_p = [sb([P, 2, 2, HALF], F32, "pair_p%d" % u) for u in range(len(units))]
+        for u, (cols, duo) in enumerate(units):
+            y1 = psum.tile([P, 2, HALF], F32, name="y1", tag="unit%d" % u)
+            for i in range(2):
+                project(y1[:, i, :], w2_q, duo.start + i, e_picked_words, e_picked_scales, E_ROW, cols)
             nc.vector.tensor_tensor(
-                pp[u][:], ys[:, t0:t1, :, c0:c1].rearrange("p t k c -> p k t c"), y[:].unsqueeze(1).to_broadcast([P, 2, nt[u], wid[u]]), MULT
+                pair_p[u][:], y02[:, duo, :, cols].rearrange("p t k c -> p k t c"), y1[:].unsqueeze(1).to_broadcast([P, 2, 2, HALF]), MULT
             )
 
-        def weights(u):
-            c0, c1, t0, t1 = units[u]
-            for i in range(nt[u]):
-                t = t0 + i
-                k = PACK // nt[u]
+        e_sum = []
+        for u, (cols, duo) in enumerate(units):
+            e_sum.append(psum.tile([P, len(blocks), P], F32, name="e_sum", tag="unit%d" % u))
+            for b, (i, c) in enumerate(blocks):
+                first = cols.start + c
+                nc.tensor.matmul(e_sum[u][:, b, :], e02[:, duo.start + i, first : first + P], ident[:], start=(b == 0), stop=False, is_transpose=True)
+
+        term02 = sb([P, PACK, S], F32, "term02", tag="e_word_table")
+        for cols, duo in units:
+            nc.gpsimd.tensor_tensor(term02[:, duo, cols], p02[:, duo, cols], e02[:, duo, cols], MULT)
+
+        recip = sb([P, PACK, S], F32, "recip")
+        pair_tanh = [sb([P, 2, PACK, P], F32, "pair_tanh%d" % u)[:] for u in range(len(units) - 1)]
+        pair_tanh.append(recip[:].rearrange("p t (h w) -> p h t w", h=2)[:, :, :, 0:P])
+        partial = sb([P, PACK, S], F32, "partial")
+        num = sb([P, PACK, S], F32, "num")
+        sum_squared = []
+        for u, (cols, duo) in enumerate(units):
+            pair_e = sb([P, 2, 2, HALF], F32, "pair_e%d" % u)
+            for i in range(2):
+                t = duo.start + i
                 nc.scalar.activation(
-                    th[u][:, :, i * k : (i + 1) * k, :], pp[u][:, :, i, :].rearrange("p h (k w) -> p h k w", k=k), ACT.Tanh, scale=att_t[:, t : t + 1]
+                    pair_tanh[u][:, :, 2 * i : 2 * i + 2, :], pair_p[u][:, :, i, :].rearrange("p k (r w) -> p k r w", w=P),
+                    ACT.Tanh, scale=att_t[:, t : t + 1],
                 )
-            nc.scalar.activation(ee[u][:].rearrange("p h i (k w) -> p h (i k) w", w=run[u]), th[u], ACT.Exp)
+            nc.scalar.activation(pair_e[:].rearrange("p k i (r w) -> p k (i r) w", w=P), pair_tanh[u], ACT.Exp)
+            pair_term = sb([P, 2, 2, HALF], F32, "pair_term%d" % u)
+            nc.vector.tensor_tensor(pair_term[:], pair_p[u][:], pair_e[:], MULT)
 
-        def numerator(u):
-            c0, c1, t0, t1 = units[u]
-            nc.vector.tensor_tensor(nn[u][:], pp[u][:], ee[u][:], MULT)
+            for k in range(2):
+                for b, (i, c) in enumerate(blocks):
+                    closes = k == 1 and b == len(blocks) - 1
+                    nc.tensor.matmul(e_sum[u][:, b, :], pair_e[:, k, i, c : c + P], ident[:], start=False, stop=closes, is_transpose=True)
+            turned_square = sb([P, len(blocks), P], F32, "turned_square%d" % u)
+            nc.scalar.activation(turned_square[:], e_sum[u][:], ACT.Square)
+            sum_squared.append(psum.tile([P, len(blocks), P], F32, name="sum_squared", tag="unit%d" % u))
+            for b in range(len(blocks)):
+                nc.tensor.transpose(sum_squared[u][:, b, :], turned_square[:, b, :], ident[:])
 
-        def numerator_a(u):
-            c0, c1, t0, t1 = units[u]
-            nc.vector.tensor_tensor(part[:, t0:t1, c0:c1], nn[u][:, 0], n02[:, t0:t1, c0:c1], ADD)
-
-        def numerator_b(u):
-            c0, c1, t0, t1 = units[u]
-            nc.vector.tensor_tensor(num[:, t0:t1, c0:c1], part[:, t0:t1, c0:c1], nn[u][:, 1], ADD)
-
-        den = {}
-        btag = ["b0", "b1", "b2", "b3", "a0"]
-
-        def blocks(u):
-            c0, c1, t0, t1 = units[u]
-            return [(i, b) for i in range(nt[u]) for b in range(wid[u] // P)]
-
-        def den_open(u):
-            c0, c1, t0, t1 = units[u]
-            den[u] = bank([P, len(blocks(u)), P], "den", btag[u])
-            for k, (i, b) in enumerate(blocks(u)):
-                nc.tensor.matmul(den[u][:, k, :], e02[:, t0 + i, c0 + b * P : c0 + (b + 1) * P], ident[:], start=(k == 0), stop=False, is_transpose=True)
-
-        def denominator(u):
-            c0, c1, t0, t1 = units[u]
-            last = len(blocks(u)) - 1
-            if OPT["wide"]:
-                for pair in range(2):
-                    for k, (i, b) in enumerate(blocks(u)):
-                        nc.tensor.matmul(den[u][:, k, :], ee[u][:, pair, i, b * P : (b + 1) * P], ident[:], start=False, stop=(pair == 1 and k == last), is_transpose=True)
-            else:
-                den[u] = bank([P, len(blocks(u)), P], "den", btag[u])
-                for k, (i, b) in enumerate(blocks(u)):
-                    terms = (e02[:, t0 + i, c0 + b * P : c0 + (b + 1) * P], ee[u][:, 0, i, b * P : (b + 1) * P], ee[u][:, 1, i, b * P : (b + 1) * P])
-                    for j in range(3):
-                        nc.tensor.matmul(den[u][:, k, :], terms[j], ident[:], start=(j == 0), stop=(j == 2), is_transpose=True)
-            nc.scalar.activation(dsq[u][:], den[u][:], ACT.Square)
-            back[u] = bank([P, last + 1, P], "back", btag[u])
-            for k in range(last + 1):
-                nc.tensor.transpose(back[u][:, k, :], dsq[u][:, k, :], ident[:])
-
-        for (c0, c1, t0, t1) in OPT["fp"]:
-            first_pair(slice(c0, c1), slice(t0, t1))
-        for u in range(nu):
-            products(u)
-        if OPT["wide"]:
-            for u in range(nu):
-                den_open(u)
-        for (c0, c1, t0, t1, eng) in OPT["fn"]:
-            first_num(slice(c0, c1), slice(t0, t1), eng)
-        for u in range(nu):
-            weights(u)
-            numerator(u)
-            denominator(u)
-            numerator_a(u)
-            numerator_b(u)
+            nc.vector.tensor_tensor(partial[:, duo, cols], pair_term[:, 0], term02[:, duo, cols], ADD)
+            nc.vector.tensor_tensor(num[:, duo, cols], partial[:, duo, cols], pair_term[:, 1], ADD)
 
         out_rows = out_0.rearrange("(p t) j -> p t j", t=PACK)
         out_words = out_1[0].rearrange("p c r -> p (c r)").bitcast(I32)
-        o_codes = sb([P, S], U32, "o_codes")
-        o_scales = sb([P, S], U8, "o_scales")
-        o = [sb([P, PACK, HALF], F32, "o%d" % h) for h in range(2)]
-        for u in range(nu):
-            c0, c1, t0, t1 = units[u]
-            h = c0 // HALF
-            nc.scalar.activation(recip[:, t0:t1, c0:c1], back[u][:].rearrange("p (i b) c -> p i (b c)", i=nt[u]), ACT.Abs_reciprocal_sqrt)
-            nc.vector.tensor_tensor(o[h][:, t0:t1, :], num[:, t0:t1, c0:c1], recip[:, t0:t1, c0:c1], MULT)
-            if t1 == PACK:
-                nc.sync.dma_start(out_rows[:, :, halves[h]], o[h][:])
-        ob = [sb([P, HALF * PACK], BF16, "ob%d" % h) for h in range(2)]
-        for q in range(4):
-            h, r = divmod(q, 2)
-            dst = ob[h][:, r * P * PACK : (r + 1) * P * PACK].rearrange("p (c i t) -> p c t i", i=4, t=PACK)
-            src = o[h][:, :, r * P : (r + 1) * P].rearrange("p t (c i) -> p c t i", i=4)
-            if OPT["oc"][q] == "S":
-                nc.scalar.copy(dst, src)
-            else:
-                nc.vector.tensor_copy(dst, src)
-            if r == 1:
-                nc.vector.quantize_mx(out=o_codes[:, halves[h]].bitcast(FP8X4), scales=o_scales[:, halves[h]], in_=ob[h][:])
-                nc.sync.dma_start(out_words[:, halves[h]], o_codes[:, halves[h]].bitcast(I32))
-        for q in range(4):
-            (nc.scalar if q % 2 else nc.sync).dma_start(out_2[0, q:16:4, :].bitcast(I32), o_scales[q:P:32, :].bitcast(I32))
+        out_codes = sb([P, S], U32, "out_codes")
+        out_scales = sb([P, S], U8, "out_scales")
+        result = [sb([P, PACK, HALF], F32, "result%d" % h) for h in range(2)]
+        for u, (cols, duo) in enumerate(units):
+            h = cols.start // HALF
+            nc.scalar.activation(recip[:, duo, cols], sum_squared[u][:].rearrange("p (i b) c -> p i (b c)", i=2), ACT.Abs_reciprocal_sqrt)
+            nc.vector.tensor_tensor(result[h][:, duo, :], num[:, duo, cols], recip[:, duo, cols], MULT)
+            if duo.stop == PACK:
+                nc.sync.dma_start(out_rows[:, :, cols], result[h][:])
+
+        for h, cols in enumerate(halves):
+            rounded = sb([P, HALF * PACK], BF16, "rounded%d" % h)
+            for c in range(0, HALF, P):
+                copy = nc.vector.tensor_copy if cols.start + c + P == S else nc.scalar.copy
+                copy(
+                    rounded[:, c * PACK : (c + P) * PACK].rearrange("p (c i t) -> p c t i", i=4, t=PACK),
+                    result[h][:, :, c : c + P].rearrange("p t (c i) -> p c t i", i=4),
+                )
+            nc.vector.quantize_mx(out=out_codes[:, cols].bitcast(FP8X4), scales=out_scales[:, cols], in_=rounded[:])
+            nc.sync.dma_start(out_words[:, cols], out_codes[:, cols].bitcast(I32))
+        for r in range(4):
+            queue = nc.scalar if r % 2 else nc.sync
+            queue.dma_start(out_2[0, r:16:4, :].bitcast(I32), out_scales[r:P:QUAD, :].bitcast(I32))

from contextlib import ExitStack

import concourse.mybir as mybir
from concourse.masks import make_identity

F32 = mybir.dt.float32
BF16 = mybir.dt.bfloat16
I32 = mybir.dt.int32
U32 = mybir.dt.uint32
U16 = mybir.dt.uint16
U8 = mybir.dt.uint8
FP8X4 = mybir.dt.float8_e4m3fn_x4
ACT = mybir.ActivationFunctionType
MULT = mybir.AluOpType.mult
ADD = mybir.AluOpType.add

P = 128
PACK = 4
K = 512
N = 512
S = 512
HALF = S // 2
QUAD = 32
LIST_ROWS = 16
X_ROW, D_ROW, E_ROW = 0, 4, 8
FLOPS = 3 * 2 * K * N * S


def tile_picked_yafm_none_po_kernel(
    tc, x_words, x_scales, e_words, e_scales, d_words, d_scales, w1, w2, w3, att, offs, item, cxt, out_0, out_1, out_2
):
    nc = tc.nc
    whole = slice(0, S)
    halves = [slice(h * HALF, (h + 1) * HALF) for h in range(2)]
    duos = [slice(2 * d, 2 * d + 2) for d in range(2)]
    units = [(cols, duo) for cols in halves for duo in duos]
    blocks = [(i, c) for i in range(2) for c in range(0, HALF, P)]

    with ExitStack() as ctx:
        keep = ctx.enter_context(tc.tile_pool(name="keep", bufs=1))
        psum = ctx.enter_context(tc.psum_pool(name="psum", bufs=1))

        def sb(shape, dtype, name, tag=None):
            return keep.tile(shape, dtype, name=name, tag=tag or name, align_bytes=64)

        def load_list(src, name):
            tile = keep.tile([P, S // LIST_ROWS], U16, name=name)
            nc.sync.dma_start(tile[:], src)
            return tile

        def cleared_scales(src, name, engine):
            tile = sb([P, src.shape[2]], U8, name)
            engine.memset(tile[:].bitcast(I32), 0)
            return tile

        def load_scales(tile, src, row0):
            for r in range(4):
                nc.sync.dma_start(tile[row0 + r : P : QUAD, :].bitcast(I32), src[0, r:16:4, :].bitcast(I32))

        def load_words(src, name):
            tile = sb([P, src.shape[2]], I32, name)
            nc.sync.dma_start(tile[:], src[0].rearrange("p n t -> p (n t)").bitcast(I32))
            return tile

        def load_weight(src, name):
            tile = sb([P, PACK, N], F32, name)
            nc.sync.dma_start(tile[:], src.rearrange("(p j) c -> p j c", j=PACK))
            return tile

        def quantise_weight(raw, name, copy, parts):
            codes = sb([P, N], U32, name + "_codes")
            scales = sb([P, N], U8, name + "_scales")
            share = PACK // parts
            for i in range(parts):
                grouped = sb([P, share * N], BF16, name + "_grouped%d" % i)
                copy(
                    grouped[:].rearrange("p (t m j) -> p m j t", t=share, j=PACK),
                    raw[:].rearrange("p j (m t) -> p m j t", t=PACK)[:, :, :, i * share : (i + 1) * share],
                )
                span = slice(i * share * P, (i + 1) * share * P)
                nc.vector.quantize_mx(out=codes[:, span].bitcast(FP8X4), scales=scales[:, span], in_=grouped[:])
            return codes, scales

        def gather(dst, window, entries, cols):
            nc.vector.tensor_copy(dst[:, cols], window.indirect(entries[:, cols.start // LIST_ROWS : cols.stop // LIST_ROWS]))

        def project(out, weight, t, words, scales, row0, cols):
            m = slice(t * P, (t + 1) * P)
            nc.tensor.matmul_mx(
                out=out, lhsT=weight[0][:, m].bitcast(FP8X4), lhsT_scale=weight[1][:, m],
                rhs=words[:, cols].bitcast(FP8X4), rhs_scale=scales[row0:P, cols], start=True, stop=True,
            )

        x_scale_table = cleared_scales(x_scales, "x_scale_table", nc.gpsimd)
        d_scale_table = cleared_scales(d_scales, "d_scale_table", nc.vector)
        e_scale_table = cleared_scales(e_scales, "e_scale_table", nc.vector)
        d_list = load_list(cxt, "d_list")
        x_list = load_list(offs, "x_list")
        load_scales(x_scale_table, x_scales, X_ROW)
        w3_raw = load_weight(w3, "w3_raw")
        load_scales(d_scale_table, d_scales, D_ROW)
        d_word_table = load_words(d_words, "d_word_table")
        w1_raw = load_weight(w1, "w1_raw")
        x_word_table = load_words(x_words, "x_word_table")
        e_list = load_list(item, "e_list")
        load_scales(e_scale_table, e_scales, E_ROW)
        w2_raw = load_weight(w2, "w2_raw")
        e_word_table = load_words(e_words, "e_word_table")
        att_t = sb([P, PACK], F32, "att_t")
        nc.gpsimd.dma_start(att_t[:], att.rearrange("(p t) o -> p (t o)", t=PACK))

        ident = sb([P, P], F32, "ident")
        make_identity(nc, ident[:])

        x_picked_scales = sb([P, S], U8, "x_picked_scales")
        x_picked_words = sb([P, S], U32, "x_picked_words")
        d_picked_scales = sb([P, S], U8, "d_picked_scales")
        d_picked_words = sb([P, S], U32, "d_picked_words")
        e_picked_scales = sb([P, S], U8, "e_picked_scales")
        e_picked_words = sb([P, S], U32, "e_picked_words")

        y02 = sb([P, PACK, 2, S], F32, "y02")
        p02 = sb([P, PACK, S], F32, "p02")
        tanh02 = sb([P, PACK, S], F32, "tanh02")
        e02 = sb([P, PACK, S], F32, "e02")

        gather(d_picked_scales, d_scale_table[:], d_list, whole)
        w3_q = quantise_weight(w3_raw, "w3", nc.scalar.copy, 1)
        gather(x_picked_scales, x_scale_table[:], x_list, whole)
        w1_q = quantise_weight(w1_raw, "w1", nc.vector.tensor_copy, 2)
        gather(d_picked_words, d_word_table[:].bitcast(U32), d_list, whole)
        gather(x_picked_words, x_word_table[:].bitcast(U32), x_list, whole)

        for t in range(PACK):
            y2 = psum.tile([P, S], F32, name="y2", tag="tile%d" % t)
            project(y2[:], w3_q, t, d_picked_words, d_picked_scales, D_ROW, whole)
            nc.scalar.copy(y02[:, t, 1, :], y2[:])
        y0 = []
        for t in range(PACK):
            y0.append(psum.tile([P, S], F32, name="y0", tag="tile%d" % t))
            project(y0[t][:], w1_q, t, x_picked_words, x_picked_scales, X_ROW, whole)
            nc.vector.tensor_tensor(p02[:, t, :], y02[:, t, 1, :], y0[t][:], MULT)

        def keep_y0(duo):
            for t in range(duo.start, duo.stop):
                nc.scalar.copy(y02[:, t, 0, :], y0[t][:])

        keep_y0(duos[0])

        gather(e_picked_scales, e_scale_table[:], e_list, whole)
        w2_q = quantise_weight(w2_raw, "w2", nc.vector.tensor_copy, 2)
        for cols in halves:
            gather(e_picked_words, e_word_table[:].bitcast(U32), e_list, cols)

        for duo in duos:
            for t in range(duo.start, duo.stop):
                nc.scalar.activation(tanh02[:, t, :], p02[:, t, :], ACT.Tanh, scale=att_t[:, t : t + 1])
            nc.scalar.activation(e02[:, duo, :], tanh02[:, duo, :], ACT.Exp)
        keep_y0(duos[1])

        pair_p = [sb([P, 2, 2, HALF], F32, "pair_p%d" % u) for u in range(len(units))]
        for u, (cols, duo) in enumerate(units):
            y1 = psum.tile([P, 2, HALF], F32, name="y1", tag="unit%d" % u)
            for i in range(2):
                project(y1[:, i, :], w2_q, duo.start + i, e_picked_words, e_picked_scales, E_ROW, cols)
            nc.vector.tensor_tensor(
                pair_p[u][:], y02[:, duo, :, cols].rearrange("p t k c -> p k t c"), y1[:].unsqueeze(1).to_broadcast([P, 2, 2, HALF]), MULT
            )

        e_sum = []
        for u, (cols, duo) in enumerate(units):
            e_sum.append(psum.tile([P, len(blocks), P], F32, name="e_sum", tag="unit%d" % u))
            for b, (i, c) in enumerate(blocks):
                first = cols.start + c
                nc.tensor.matmul(e_sum[u][:, b, :], e02[:, duo.start + i, first : first + P], ident[:], start=(b == 0), stop=False, is_transpose=True)

        term02 = sb([P, PACK, S], F32, "term02", tag="e_word_table")
        for cols, duo in units:
            nc.gpsimd.tensor_tensor(term02[:, duo, cols], p02[:, duo, cols], e02[:, duo, cols], MULT)

        recip = sb([P, PACK, S], F32, "recip")
        pair_tanh = [sb([P, 2, PACK, P], F32, "pair_tanh%d" % u)[:] for u in range(len(units) - 1)]
        pair_tanh.append(recip[:].rearrange("p t (h w) -> p h t w", h=2)[:, :, :, 0:P])
        partial = sb([P, PACK, S], F32, "partial")
        num = sb([P, PACK, S], F32, "num")
        sum_squared = []
        for u, (cols, duo) in enumerate(units):
            pair_e = sb([P, 2, 2, HALF], F32, "pair_e%d" % u)
            for i in range(2):
                t = duo.start + i
                nc.scalar.activation(
                    pair_tanh[u][:, :, 2 * i : 2 * i + 2, :], pair_p[u][:, :, i, :].rearrange("p k (r w) -> p k r w", w=P),
                    ACT.Tanh, scale=att_t[:, t : t + 1],
                )
            nc.scalar.activation(pair_e[:].rearrange("p k i (r w) -> p k (i r) w", w=P), pair_tanh[u], ACT.Exp)
            pair_term = sb([P, 2, 2, HALF], F32, "pair_term%d" % u)
            nc.vector.tensor_tensor(pair_term[:], pair_p[u][:], pair_e[:], MULT)

            for k in range(2):
                for b, (i, c) in enumerate(blocks):
                    closes = k == 1 and b == len(blocks) - 1
                    nc.tensor.matmul(e_sum[u][:, b, :], pair_e[:, k, i, c : c + P], ident[:], start=False, stop=closes, is_transpose=True)
            turned_square = sb([P, len(blocks), P], F32, "turned_square%d" % u)
            nc.scalar.activation(turned_square[:], e_sum[u][:], ACT.Square)
            sum_squared.append(psum.tile([P, len(blocks), P], F32, name="sum_squared", tag="unit%d" % u))
            for b in range(len(blocks)):
                nc.tensor.transpose(sum_squared[u][:, b, :], turned_square[:, b, :], ident[:])

            nc.vector.tensor_tensor(partial[:, duo, cols], pair_term[:, 0], term02[:, duo, cols], ADD)
            nc.vector.tensor_tensor(num[:, duo, cols], partial[:, duo, cols], pair_term[:, 1], ADD)

        out_rows = out_0.rearrange("(p t) j -> p t j", t=PACK)
        out_words = out_1[0].rearrange("p c r -> p (c r)").bitcast(I32)
        out_codes = sb([P, S], U32, "out_codes")
        out_scales = sb([P, S], U8, "out_scales")
        result = [sb([P, PACK, HALF], F32, "result%d" % h) for h in range(2)]
        for u, (cols, duo) in enumerate(units):
            h = cols.start // HALF
            nc.scalar.activation(recip[:, duo, cols], sum_squared[u][:].rearrange("p (i b) c -> p i (b c)", i=2), ACT.Abs_reciprocal_sqrt)
            nc.vector.tensor_tensor(result[h][:, duo, :], num[:, duo, cols], recip[:, duo, cols], MULT)
            if duo.stop == PACK:
                nc.sync.dma_start(out_rows[:, :, cols], result[h][:])

        for h, cols in enumerate(halves):
            rounded = sb([P, HALF * PACK], BF16, "rounded%d" % h)
            for c in range(0, HALF, P):
                copy = nc.vector.tensor_copy if cols.start + c + P == S else nc.scalar.copy
                copy(
                    rounded[:, c * PACK : (c + P) * PACK].rearrange("p (c i t) -> p c t i", i=4, t=PACK),
                    result[h][:, :, c : c + P].rearrange("p t (c i) -> p c t i", i=4),
                )
            nc.vector.quantize_mx(out=out_codes[:, cols].bitcast(FP8X4), scales=out_scales[:, cols], in_=rounded[:])
            nc.sync.dma_start(out_words[:, cols], out_codes[:, cols].bitcast(I32))
        for r in range(4):
            queue = nc.scalar if r % 2 else nc.sync
            queue.dma_start(out_2[0, r:16:4, :].bitcast(I32), out_scales[r:P:QUAD, :].bitcast(I32))
